import numpy as np
import ml_dtypes


def mxq(x, axis, fmt="e4m3"):
    dtype, down = {"e4m3": (ml_dtypes.float8_e4m3fn, 7), "e5m2": (ml_dtypes.float8_e5m2, 14)}[fmt]
    v = np.moveaxis(np.asarray(x, np.float32).astype(ml_dtypes.bfloat16).astype(np.float64), axis, -1)
    blocks = v.reshape(v.shape[:-1] + (-1, 32))
    amax = np.abs(blocks).max(-1, keepdims=True)
    byte = np.maximum(np.where(amax > 0, np.frexp(amax)[1] - 1 + 127, 0) - down, 1)
    scale = np.exp2(byte - 127.0)
    codes = (blocks / scale).astype(np.float32).astype(dtype).astype(np.float64)
    return np.moveaxis((codes * scale).reshape(v.shape), -1, axis)


WIDE = False


def mx_kscale(k):
    if not WIDE:
        return np.ones(k)
    levels = np.array([30, -30])
    if k % 512:
        return np.exp2(np.random.permutation(np.resize(levels, k // 32))).repeat(32)
    a = np.empty((k // 512, 16))
    for p in range(k // 512):
        a[p, :8] = np.random.permutation(np.resize(levels, 8))
        for g in range(8):
            far = levels[np.abs(levels - a[p, g]) >= 10]
            a[p, g + 8] = far[np.random.randint(len(far))]
    return np.exp2(a.ravel()).repeat(32)


BF16 = ml_dtypes.bfloat16


def bf(x):
    return np.asarray(x, np.float32).astype(BF16)


def f64(x):
    return np.asarray(x).astype(np.float64)


E2M1 = np.array([0.0, 0.5, 1.0, 1.5, 2.0, 3.0, 4.0, 6.0, -0.0, -0.5, -1.0, -1.5, -2.0, -3.0, -4.0, -6.0])


def pack_weight(w, fmt):
    k, n = w.shape
    w = f64(bf(w)).reshape(k // 32, 32, n)
    amax = np.abs(w).max(1)
    if fmt in ("e4m3", "e5m2"):
        byte = np.frexp(amax)[1] - 1 + 127 - (7 if fmt == "e4m3" else 14)
    else:
        mant, ex = np.frexp(amax / 6.0)
        byte = np.where(mant > 0.5, ex, ex - 1) + 127
    byte = np.clip(np.where(amax > 0, byte, 1), 1, 254)
    scaled = (w * np.exp2(127.0 - byte)[:, None, :]).reshape(k, n).astype(np.float32)
    by_word = np.ascontiguousarray(scaled.reshape(k // 512, 128, 4, n).transpose(0, 1, 3, 2))
    if fmt in ("e4m3", "e5m2"):
        words = by_word.astype(ml_dtypes.float8_e4m3fn if fmt == "e4m3" else ml_dtypes.float8_e5m2).view(np.uint8)
    else:
        c = by_word.astype(ml_dtypes.float4_e2m1fn).view(np.uint8) & 0xF
        words = c[..., 0::2] | (c[..., 1::2] << 4)
    return np.ascontiguousarray(words), np.ascontiguousarray(byte.astype(np.uint8).reshape(k // 512, 16, n))


def unpack_weight(words, scales, fmt):
    g, p, n, _ = words.shape
    if fmt in ("e4m3", "e5m2"):
        vals = np.ascontiguousarray(words).view(ml_dtypes.float8_e4m3fn if fmt == "e4m3" else ml_dtypes.float8_e5m2).astype(np.float64)
    else:
        nib = np.empty((g, p, n, 4), np.uint8)
        nib[..., 0::2] = words & 0xF
        nib[..., 1::2] = words >> 4
        vals = E2M1[nib]
    vals = vals * np.repeat(np.exp2(scales.astype(np.float64) - 127.0), 8, axis=1)[..., None]
    return vals.transpose(0, 1, 3, 2).reshape(g * 512, n)


K, C, N = 2048, 1536, 1024


def setup_inputs():
    s = mx_kscale(K)
    g = np.random.standard_normal((K, N)) * np.exp(0.7 * np.random.standard_normal((K, N)))
    g_words, g_scales = pack_weight(g * s[:, None], "e5m2")
    jac = np.random.standard_normal((K, C)) / np.sqrt(K) / s[:, None]
    return {"g_words": g_words,
            "g_scales": g_scales,
            "jac": bf(jac),
            "e_scale": bf(1 + 0.1 * np.random.standard_normal(N)),
            "base": bf(0.3 * np.random.standard_normal(C))}


def reference(g_words, g_scales, jac, e_scale, base):
    g = unpack_weight(g_words, g_scales, "e5m2")
    j = mxq(f64(jac), 0, "e4m3")
    grad = j.T @ g
    return f64(base)[:, None] - grad * f64(e_scale)[None, :]

@@ -1,0 +1,190 @@
+from contextlib import ExitStack
+
+import concourse.mybir as mybir
+from concourse.masks import make_identity
+
+K, C, N = 2048, 1536, 1024
+FLOPS = 2 * K * C * N
+
+F32 = mybir.dt.float32
+BF16 = mybir.dt.bfloat16
+I32 = mybir.dt.int32
+U32 = mybir.dt.uint32
+U8 = mybir.dt.uint8
+E4M3X4 = mybir.dt.float8_e4m3fn_x4
+E5M2X4 = mybir.dt.float8_e5m2_x4
+ACT = mybir.ActivationFunctionType
+ALU = mybir.AluOpType
+
+P = 128
+PACK = 4
+K_PASS = P * PACK
+PASSES = K // K_PASS
+CHUNK = 512
+STRIP = 256
+NH = 512
+BANKS = 8
+LEAD = 5
+ADD_LAG = 2
+VECTOR_ADDS = (17, 19, 21, 23)
+
+
+def tile_committee_descriptor_forces_e1_kernel(tc, g_words, g_scales, jac, e_scale, base, out):
+    nc = tc.nc
+    with ExitStack() as ctx:
+        sb = ctx.enter_context(tc.tile_pool(name="sb", bufs=1))
+        ps = ctx.enter_context(tc.psum_pool(name="ps", bufs=1))
+        ctx.enter_context(tc.manual_schedule())
+
+        banks = [ps.tile([P, NH], F32, name="bank%d" % b) for b in range(BANKS)]
+        raw, grouped, j_codes, j_scales = {}, {}, {}, {}
+        for ch in range(C // CHUNK):
+            for g in range(PASSES):
+                raw[ch, g] = sb.tile([P, PACK, CHUNK], BF16, name="raw%d_%d" % (ch, g), align_bytes=64)
+                for s in range(2):
+                    key = (2 * ch + s, g)
+                    grouped[key] = sb.tile([P, STRIP, PACK], BF16, name="grp%d_%d" % key, align_bytes=64)
+                    j_codes[key] = sb.tile([P, STRIP], U32, name="jc%d_%d" % key, align_bytes=64)
+                    j_scales[key] = sb.tile([P, STRIP], U8, name="js%d_%d" % key, align_bytes=64)
+        g_codes = {}
+        for h in range(2):
+            for g in range(PASSES):
+                g_codes[g, h] = sb.tile([P, NH], U32, name="gc%d_%d" % (g, h), align_bytes=64)
+        g_plane = [sb.tile([P, PASSES * NH], U8, name="gs%d" % h, align_bytes=64) for h in range(2)]
+        neg_e = [sb.tile([P, NH], F32, name="nege%d" % h) for h in range(2)]
+        e_rows = sb.tile([P, 2, PACK], BF16)
+        base_rows = sb.tile([P, P], BF16)
+        base_cols = sb.tile([P, C // P], F32)
+        ident32 = sb.tile([P, P], F32)
+        ident = sb.tile([P, P], BF16)
+
+        groups = [(t, 0) for t in range(BANKS)] + [(t, 1) for t in range(BANKS)]
+        groups += [(t, h) for t in range(BANKS, C // P) for h in range(2)]
+        res = [sb.tile([P, NH], F32, name="res%d" % i) for i in range(len(groups))]
+
+        def load_jac(ch, g):
+            rows = jac[g * K_PASS:(g + 1) * K_PASS, ch * CHUNK:(ch + 1) * CHUNK]
+            nc.sync.dma_start(out=raw[ch, g][:], in_=rows.rearrange("(p j) w -> p j w", j=PACK))
+
+        def load_g(g, h):
+            words = g_words[g].rearrange("p n t -> p (n t)")[:, h * NH * PACK:(h + 1) * NH * PACK]
+            nc.sync.dma_start(out=g_codes[g, h][:].bitcast(I32), in_=words.bitcast(I32))
+
+        def load_g_scales(h):
+            dst = g_plane[h][:].bitcast(I32).rearrange("p (g w) -> p g w", g=PASSES)
+            src = g_scales.rearrange("g (q r) n -> r q g n", r=4)
+            for r in range(4):
+                nc.sync.dma_start(out=dst[r:P:32], in_=src[r][:, :, h * NH:(h + 1) * NH].bitcast(I32))
+
+        def interleave(on_vector, strip, g, c0, width):
+            first = (strip % 2) * STRIP + c0
+            src = raw[strip // 2, g][:, :, first:first + width].rearrange("p t (c i) -> p c t i", i=4)
+            dst = grouped[strip, g][:, c0:c0 + width, :].rearrange("p (c i) t -> p c t i", i=4)
+            if on_vector:
+                nc.vector.tensor_copy(out=dst, in_=src)
+            else:
+                nc.scalar.copy(out=dst, in_=src)
+
+        def quantize(strip, g):
+            nc.vector.quantize_mx(
+                out=j_codes[strip, g][:].bitcast(E4M3X4),
+                scales=j_scales[strip, g][:],
+                in_=grouped[strip, g][:].rearrange("p c t -> p (c t)"),
+            )
+
+        def multiply(i, g):
+            t, h = groups[i]
+            cols = slice((t % 2) * P, (t % 2 + 1) * P)
+            nc.tensor.matmul_mx(
+                out=banks[i % BANKS][:],
+                lhsT=j_codes[t // 2, g][:, cols].bitcast(E4M3X4),
+                lhsT_scale=j_scales[t // 2, g][:, cols],
+                rhs=g_codes[g, h][:].bitcast(E5M2X4),
+                rhs_scale=g_plane[h][:, g * NH:(g + 1) * NH],
+                start=(g == 0),
+                stop=(g == PASSES - 1),
+            )
+
+        def scale_out(i):
+            nc.vector.tensor_tensor(out=res[i][:], in0=banks[i % BANKS][:], in1=neg_e[groups[i][1]][:], op=ALU.mult)
+
+        def finish(i):
+            t, h = groups[i]
+            if i in VECTOR_ADDS:
+                nc.vector.tensor_scalar_add(out=res[i][:], in0=res[i][:], scalar1=base_cols[:, t:t + 1])
+            else:
+                nc.scalar.activation(out=res[i][:], in_=res[i][:], func=ACT.Identity, bias=base_cols[:, t:t + 1])
+            nc.sync.dma_start(out=out[t * P:(t + 1) * P, h * NH:(h + 1) * NH], in_=res[i][:])
+
+        nc.scalar.dma_start(out=e_rows[:], in_=e_scale.rearrange("(h q m) -> q h m", h=2, m=PACK))
+        for h in range(2):
+            nc.vector.memset(g_plane[h][:].bitcast(I32), 0)
+        nc.gpsimd.memset(base_rows[:], 0.0)
+        make_identity(nc, ident32[:])
+        nc.scalar.dma_start(out=base_rows[0:C // P, :], in_=base.rearrange("(t p) -> t p", p=P))
+        nc.scalar.activation(out=ident[:], in_=ident32[:], func=ACT.Identity)
+
+        load_jac(0, 0)
+        load_g_scales(0)
+        load_g(0, 0)
+        load_jac(1, 0)
+        for g in range(1, PASSES - 1):
+            load_jac(0, g)
+            load_g(g, 0)
+            load_jac(1, g)
+        load_jac(0, PASSES - 1)
+        load_jac(1, PASSES - 1)
+        load_g(PASSES - 1, 0)
+        load_g_scales(1)
+        for g in range(PASSES):
+            load_g(g, 1)
+        for g in range(PASSES):
+            load_jac(2, g)
+
+        spread = [banks[BANKS - 2 + h][:].bitcast(BF16) for h in range(2)]
+        for h in range(2):
+            for m in range(PACK):
+                nc.tensor.transpose(
+                    spread[h][:, m * P:(m + 1) * P], e_rows[:, h, m:m + 1].to_broadcast([P, P]), ident[:]
+                )
+        nc.tensor.transpose(spread[0][:, NH:NH + P], base_rows[:], ident[:])
+        e_src = [spread[h][:, 0:NH].rearrange("p (m q) -> p q m", m=PACK) for h in range(2)]
+        e_dst = [neg_e[h][:].rearrange("p (q m) -> p q m", m=PACK) for h in range(2)]
+        nc.vector.tensor_scalar_mul(out=e_dst[0], in0=e_src[0], scalar1=-1.0)
+        nc.scalar.activation(out=e_dst[1], in_=e_src[1], func=ACT.Identity, scale=-1.0)
+        nc.vector.tensor_copy(out=base_cols[:], in_=spread[0][:, NH:NH + C // P])
+
+        def strip_ready(strip, g):
+            quantize(strip, g)
+            multiply(2 * strip, g)
+            multiply(2 * strip + 1, g)
+
+        pending = None
+        for g in range(PASSES):
+            for ch in range(2):
+                interleave(True, 2 * ch, g, 0, STRIP)
+                interleave(False, 2 * ch + 1, g, 0, STRIP)
+                if pending is not None:
+                    strip_ready(*pending)
+                strip_ready(2 * ch, g)
+                pending = (2 * ch + 1, g)
+        strip_ready(*pending)
+
+        late = [(strip, g) for strip in (4, 5) for g in range(PASSES)]
+        for i in range(len(groups) + ADD_LAG):
+            j = i - LEAD
+            prepare = 0 <= j < len(late)
+            if prepare:
+                interleave(True, late[j][0], late[j][1], 0, P)
+                interleave(False, late[j][0], late[j][1], P, P)
+            if i < len(groups):
+                scale_out(i)
+            if prepare:
+                quantize(*late[j])
+            if i >= ADD_LAG and i - ADD_LAG not in VECTOR_ADDS:
+                finish(i - ADD_LAG)
+            if i - 1 in VECTOR_ADDS:
+                finish(i - 1)
+            if i + BANKS < len(groups):
+                for g in range(PASSES):
+                    multiply(i + BANKS, g)

@@ -24,9 +24,11 @@ CHUNK = 512
 STRIP = 256
 NH = 512
 BANKS = 8
-LEAD = 5
+PREP_STEPS = (7, 8, 9, 10, 12, 13, 14, 15)
+LATE_SPLIT = 128
 ADD_LAG = 2
-VECTOR_ADDS = (17, 19, 21, 23)
+SINGLE_STORES = 2
+VECTOR_ADDS = ()
 
 
 def tile_committee_descriptor_forces_e1_kernel(tc, g_words, g_scales, jac, e_scale, base, out):
@@ -47,28 +49,32 @@ def tile_committee_descriptor_forces_e1_kernel(tc, g_words, g_scales, jac, e_sca
                     j_codes[key] = sb.tile([P, STRIP], U32, name="jc%d_%d" % key, align_bytes=64)
                     j_scales[key] = sb.tile([P, STRIP], U8, name="js%d_%d" % key, align_bytes=64)
         g_codes = {}
-        for h in range(2):
-            for g in range(PASSES):
-                g_codes[g, h] = sb.tile([P, NH], U32, name="gc%d_%d" % (g, h), align_bytes=64)
+        g_late = sb.tile([P, PASSES, NH], U32, align_bytes=64)
+        for g in range(PASSES):
+            g_codes[g, 0] = sb.tile([P, NH], U32, name="gc%d" % g, align_bytes=64)[:]
+            g_codes[g, 1] = g_late[:, g, :]
         g_plane = [sb.tile([P, PASSES * NH], U8, name="gs%d" % h, align_bytes=64) for h in range(2)]
         neg_e = [sb.tile([P, NH], F32, name="nege%d" % h) for h in range(2)]
         e_rows = sb.tile([P, 2, PACK], BF16)
         base_rows = sb.tile([P, P], BF16)
         base_cols = sb.tile([P, C // P], F32)
-        ident32 = sb.tile([P, P], F32)
+        one = sb.tile([P, 1], F32)
+        minus_one = sb.tile([P, 1], F32)
         ident = sb.tile([P, P], BF16)
 
         groups = [(t, 0) for t in range(BANKS)] + [(t, 1) for t in range(BANKS)]
         groups += [(t, h) for t in range(BANKS, C // P) for h in range(2)]
-        res = [sb.tile([P, NH], F32, name="res%d" % i) for i in range(len(groups))]
+        pairs = [sb.tile([P, 2, NH], F32, name="res%d" % i) for i in range(len(groups) // 2)]
+        res = [pairs[i // 2][:, i % 2, :] for i in range(len(groups))]
 
         def load_jac(ch, g):
             rows = jac[g * K_PASS:(g + 1) * K_PASS, ch * CHUNK:(ch + 1) * CHUNK]
             nc.sync.dma_start(out=raw[ch, g][:], in_=rows.rearrange("(p j) w -> p j w", j=PACK))
 
-        def load_g(g, h):
-            words = g_words[g].rearrange("p n t -> p (n t)")[:, h * NH * PACK:(h + 1) * NH * PACK]
-            nc.sync.dma_start(out=g_codes[g, h][:].bitcast(I32), in_=words.bitcast(I32))
+        g_rows = g_words.rearrange("g p n t -> p g (n t)").bitcast(I32)
+
+        def load_g(g):
+            nc.sync.dma_start(out=g_codes[g, 0].bitcast(I32), in_=g_rows[:, g, 0:NH])
 
         def load_g_scales(h):
             dst = g_plane[h][:].bitcast(I32).rearrange("p (g w) -> p g w", g=PASSES)
@@ -99,45 +105,47 @@ def tile_committee_descriptor_forces_e1_kernel(tc, g_words, g_scales, jac, e_sca
                 out=banks[i % BANKS][:],
                 lhsT=j_codes[t // 2, g][:, cols].bitcast(E4M3X4),
                 lhsT_scale=j_scales[t // 2, g][:, cols],
-                rhs=g_codes[g, h][:].bitcast(E5M2X4),
+                rhs=g_codes[g, h].bitcast(E5M2X4),
                 rhs_scale=g_plane[h][:, g * NH:(g + 1) * NH],
                 start=(g == 0),
                 stop=(g == PASSES - 1),
             )
 
         def scale_out(i):
-            nc.vector.tensor_tensor(out=res[i][:], in0=banks[i % BANKS][:], in1=neg_e[groups[i][1]][:], op=ALU.mult)
+            nc.vector.tensor_tensor(out=res[i], in0=banks[i % BANKS][:], in1=neg_e[groups[i][1]][:], op=ALU.mult)
 
         def finish(i):
             t, h = groups[i]
             if i in VECTOR_ADDS:
-                nc.vector.tensor_scalar_add(out=res[i][:], in0=res[i][:], scalar1=base_cols[:, t:t + 1])
+                nc.vector.tensor_scalar_add(out=res[i], in0=res[i], scalar1=base_cols[:, t:t + 1])
             else:
-                nc.scalar.activation(out=res[i][:], in_=res[i][:], func=ACT.Identity, bias=base_cols[:, t:t + 1])
-            nc.sync.dma_start(out=out[t * P:(t + 1) * P, h * NH:(h + 1) * NH], in_=res[i][:])
+                nc.scalar.activation(out=res[i], in_=res[i], func=ACT.Identity, bias=base_cols[:, t:t + 1])
+            if i >= len(groups) - SINGLE_STORES:
+                nc.sync.dma_start(out=out[t * P:(t + 1) * P, h * NH:(h + 1) * NH], in_=res[i])
+            elif i % 2 == 1 and i < 2 * BANKS:
+                rows = out[(t - 1) * P:(t + 1) * P, h * NH:(h + 1) * NH]
+                nc.sync.dma_start(out=rows.rearrange("(u p) n -> p u n", p=P), in_=pairs[i // 2][:])
+            elif i % 2 == 1:
+                nc.sync.dma_start(out=out[t * P:(t + 1) * P, :], in_=pairs[i // 2][:].rearrange("p u n -> p (u n)"))
 
         nc.scalar.dma_start(out=e_rows[:], in_=e_scale.rearrange("(h q m) -> q h m", h=2, m=PACK))
+        nc.vector.memset(one[:], 1.0)
+        nc.vector.memset(base_rows[:], 0.0)
+        nc.scalar.activation(out=minus_one[:], in_=one[:], func=ACT.Identity, scale=-1.0)
+        nc.gpsimd.dma_start(out=base_rows[0:C // P, :], in_=base.rearrange("(t p) -> t p", p=P))
         for h in range(2):
             nc.vector.memset(g_plane[h][:].bitcast(I32), 0)
-        nc.gpsimd.memset(base_rows[:], 0.0)
-        make_identity(nc, ident32[:])
-        nc.scalar.dma_start(out=base_rows[0:C // P, :], in_=base.rearrange("(t p) -> t p", p=P))
-        nc.scalar.activation(out=ident[:], in_=ident32[:], func=ACT.Identity)
+        make_identity(nc, ident[:])
 
-        load_jac(0, 0)
-        load_g_scales(0)
-        load_g(0, 0)
-        load_jac(1, 0)
-        for g in range(1, PASSES - 1):
-            load_jac(0, g)
-            load_g(g, 0)
-            load_jac(1, g)
-        load_jac(0, PASSES - 1)
-        load_jac(1, PASSES - 1)
-        load_g(PASSES - 1, 0)
-        load_g_scales(1)
         for g in range(PASSES):
-            load_g(g, 1)
+            load_jac(0, g)
+            load_jac(1, g)
+            if g == 0:
+                load_g_scales(0)
+            load_g(g)
+        load_g_scales(1)
+        for g in range(0, PASSES, 2):
+            nc.sync.dma_start(out=g_late[:, g:g + 2, :].bitcast(I32), in_=g_rows[:, g:g + 2, NH:N])
         for g in range(PASSES):
             load_jac(2, g)
 
@@ -148,43 +156,67 @@ def tile_committee_descriptor_forces_e1_kernel(tc, g_words, g_scales, jac, e_sca
                     spread[h][:, m * P:(m + 1) * P], e_rows[:, h, m:m + 1].to_broadcast([P, P]), ident[:]
                 )
         nc.tensor.transpose(spread[0][:, NH:NH + P], base_rows[:], ident[:])
-        e_src = [spread[h][:, 0:NH].rearrange("p (m q) -> p q m", m=PACK) for h in range(2)]
-        e_dst = [neg_e[h][:].rearrange("p (q m) -> p q m", m=PACK) for h in range(2)]
-        nc.vector.tensor_scalar_mul(out=e_dst[0], in0=e_src[0], scalar1=-1.0)
-        nc.scalar.activation(out=e_dst[1], in_=e_src[1], func=ACT.Identity, scale=-1.0)
-        nc.vector.tensor_copy(out=base_cols[:], in_=spread[0][:, NH:NH + C // P])
 
-        def strip_ready(strip, g):
-            quantize(strip, g)
+        def fetch_constants():
+            e_src = [spread[h][:, 0:NH].rearrange("p (m q) -> p q m", m=PACK) for h in range(2)]
+            e_dst = [neg_e[h][:].rearrange("p (q m) -> p q m", m=PACK) for h in range(2)]
+            nc.vector.tensor_scalar_mul(out=e_dst[0], in0=e_src[0], scalar1=minus_one[:])
+            nc.scalar.activation(out=e_dst[1], in_=e_src[1], func=ACT.Identity, scale=minus_one[:])
+            nc.vector.tensor_copy(out=base_cols[:], in_=spread[0][:, NH:NH + C // P])
+
+        def multiply_strip(strip, g):
             multiply(2 * strip, g)
             multiply(2 * strip + 1, g)
 
-        pending = None
         for g in range(PASSES):
-            for ch in range(2):
-                interleave(True, 2 * ch, g, 0, STRIP)
-                interleave(False, 2 * ch + 1, g, 0, STRIP)
-                if pending is not None:
-                    strip_ready(*pending)
-                strip_ready(2 * ch, g)
-                pending = (2 * ch + 1, g)
-        strip_ready(*pending)
+            interleave(True, 0, g, 0, STRIP)
+            interleave(False, 1, g, 0, STRIP)
+            quantize(0, g)
+            interleave(True, 2, g, 0, STRIP)
+            interleave(False, 3, g, 0, STRIP)
+            quantize(1, g)
+            quantize(2, g)
+            if g == 0:
+                fetch_constants()
+            quantize(3, g)
+            for strip in range(4):
+                multiply_strip(strip, g)
 
         late = [(strip, g) for strip in (4, 5) for g in range(PASSES)]
-        for i in range(len(groups) + ADD_LAG):
-            j = i - LEAD
-            prepare = 0 <= j < len(late)
+        last = len(groups) - 1
+        issued = BANKS
+        quantized = set((strip, PASSES - 1) for strip in range(4))
+        for i in range(last + ADD_LAG):
+            prepare = i in PREP_STEPS
             if prepare:
-                interleave(True, late[j][0], late[j][1], 0, P)
-                interleave(False, late[j][0], late[j][1], P, P)
-            if i < len(groups):
+                j = PREP_STEPS.index(i)
+                interleave(True, late[j][0], late[j][1], 0, LATE_SPLIT)
+                interleave(False, late[j][0], late[j][1], LATE_SPLIT, STRIP - LATE_SPLIT)
+            if i < last:
                 scale_out(i)
             if prepare:
                 quantize(*late[j])
+                quantized.add(late[j])
             if i >= ADD_LAG and i - ADD_LAG not in VECTOR_ADDS:
                 finish(i - ADD_LAG)
             if i - 1 in VECTOR_ADDS:
                 finish(i - 1)
-            if i + BANKS < len(groups):
+            while issued <= min(i + BANKS, last) and (groups[issued][0] // 2, PASSES - 1) in quantized:
                 for g in range(PASSES):
-                    multiply(i + BANKS, g)
+                    multiply(issued, g)
+                issued += 1
+
+        t, h = groups[last]
+        for u in range(2):
+            cols = slice(u * NH // 2, (u + 1) * NH // 2)
+            nc.vector.tensor_tensor(out=res[last][:, cols], in0=banks[last % BANKS][:, cols], in1=neg_e[h][:, cols], op=ALU.mult)
+        for u in range(2):
+            cols = slice(u * NH // 2, (u + 1) * NH // 2)
+            part = res[last][:, cols]
+            rows = out[t * P:(t + 1) * P, h * NH + cols.start:h * NH + cols.stop]
+            if u == 0:
+                nc.scalar.activation(out=part, in_=part, func=ACT.Identity, bias=base_cols[:, t:t + 1])
+                nc.scalar.dma_start(out=rows, in_=part)
+            else:
+                nc.vector.tensor_scalar_add(out=part, in0=part, scalar1=base_cols[:, t:t + 1])
+                nc.sync.dma_start(out=rows, in_=part)

@@ -20,15 +20,17 @@ P = 128
 PACK = 4
 K_PASS = P * PACK
 PASSES = K // K_PASS
-CHUNK = 512
-STRIP = 256
-NH = 512
+TILES = C // P
+STRIP = 2 * P
+STRIPS = C // STRIP
+HALF = N // 2
 BANKS = 8
-PREP_STEPS = (7, 8, 9, 10, 12, 13, 14, 15)
-LATE_SPLIT = 128
+FIRST_STRIPS = BANKS // 2
+RUN = 4
+SCALE_ROWS = 4
 ADD_LAG = 2
-SINGLE_STORES = 2
-VECTOR_ADDS = ()
+OPENING_GROUPS = 2
+SINGLE_STORES = 4
 
 
 def tile_committee_descriptor_forces_e1_kernel(tc, g_words, g_scales, jac, e_scale, base, out):
@@ -38,64 +40,64 @@ def tile_committee_descriptor_forces_e1_kernel(tc, g_words, g_scales, jac, e_sca
         ps = ctx.enter_context(tc.psum_pool(name="ps", bufs=1))
         ctx.enter_context(tc.manual_schedule())
 
-        banks = [ps.tile([P, NH], F32, name="bank%d" % b) for b in range(BANKS)]
-        raw, grouped, j_codes, j_scales = {}, {}, {}, {}
-        for ch in range(C // CHUNK):
+        banks = [ps.tile([P, HALF], F32, name="bank%d" % b) for b in range(BANKS)]
+        jac_rows, side_by_side, jac_codes, jac_scales = {}, {}, {}, {}
+        for strip in range(STRIPS):
             for g in range(PASSES):
-                raw[ch, g] = sb.tile([P, PACK, CHUNK], BF16, name="raw%d_%d" % (ch, g), align_bytes=64)
-                for s in range(2):
-                    key = (2 * ch + s, g)
-                    grouped[key] = sb.tile([P, STRIP, PACK], BF16, name="grp%d_%d" % key, align_bytes=64)
-                    j_codes[key] = sb.tile([P, STRIP], U32, name="jc%d_%d" % key, align_bytes=64)
-                    j_scales[key] = sb.tile([P, STRIP], U8, name="js%d_%d" % key, align_bytes=64)
+                key = (strip, g)
+                side_by_side[key] = sb.tile([P, STRIP, PACK], BF16, name="side%d_%d" % key, align_bytes=64)
+                jac_codes[key] = sb.tile([P, STRIP], U32, name="jcode%d_%d" % key, align_bytes=64)
+                jac_scales[key] = sb.tile([P, STRIP], U8, name="jscale%d_%d" % key, align_bytes=64)
+        g_second = sb.tile([P, PASSES, HALF], U32, align_bytes=64)
         g_codes = {}
-        g_late = sb.tile([P, PASSES, NH], U32, align_bytes=64)
         for g in range(PASSES):
-            g_codes[g, 0] = sb.tile([P, NH], U32, name="gc%d" % g, align_bytes=64)[:]
-            g_codes[g, 1] = g_late[:, g, :]
-        g_plane = [sb.tile([P, PASSES * NH], U8, name="gs%d" % h, align_bytes=64) for h in range(2)]
-        neg_e = [sb.tile([P, NH], F32, name="nege%d" % h) for h in range(2)]
-        e_rows = sb.tile([P, 2, PACK], BF16)
+            g_codes[g, 0] = sb.tile([P, HALF], U32, name="gfirst%d" % g, align_bytes=64)[:]
+            g_codes[g, 1] = g_second[:, g, :]
+        g_scale_tiles = [sb.tile([P, PASSES * HALF], U8, name="gscale%d" % h, align_bytes=64) for h in range(2)]
+        neg_e = [sb.tile([P, HALF], F32, name="nege%d" % h) for h in range(2)]
+        e_parts = sb.tile([P, 2, PACK], BF16)
         base_rows = sb.tile([P, P], BF16)
-        base_cols = sb.tile([P, C // P], F32)
+        base_cols = sb.tile([P, TILES], F32)
         one = sb.tile([P, 1], F32)
         minus_one = sb.tile([P, 1], F32)
         ident = sb.tile([P, P], BF16)
 
         groups = [(t, 0) for t in range(BANKS)] + [(t, 1) for t in range(BANKS)]
-        groups += [(t, h) for t in range(BANKS, C // P) for h in range(2)]
-        pairs = [sb.tile([P, 2, NH], F32, name="res%d" % i) for i in range(len(groups) // 2)]
-        res = [pairs[i // 2][:, i % 2, :] for i in range(len(groups))]
+        groups += [(t, h) for t in range(BANKS, TILES) for h in range(2)]
+        last = len(groups) - 1
+        pairs = [sb.tile([P, 2, HALF], F32, name="result%d" % u) for u in range(len(groups) // 2)]
+        results = [pairs[i // 2][:, i % 2, :] for i in range(len(groups))]
 
-        def load_jac(ch, g):
-            rows = jac[g * K_PASS:(g + 1) * K_PASS, ch * CHUNK:(ch + 1) * CHUNK]
-            nc.sync.dma_start(out=raw[ch, g][:], in_=rows.rearrange("(p j) w -> p j w", j=PACK))
+        g_word_rows = g_words.rearrange("g p n j -> p g (n j)").bitcast(I32)
 
-        g_rows = g_words.rearrange("g p n t -> p g (n t)").bitcast(I32)
-
-        def load_g(g):
-            nc.sync.dma_start(out=g_codes[g, 0].bitcast(I32), in_=g_rows[:, g, 0:NH])
+        def load_strip_pair(strip, g):
+            rows = jac[g * K_PASS:(g + 1) * K_PASS, strip * STRIP:(strip + 2) * STRIP]
+            staged = sb.tile([P, PACK, 2 * STRIP], BF16, name="rows%d_%d" % (strip, g), align_bytes=64)
+            jac_rows[strip, g] = staged[:, :, 0:STRIP]
+            jac_rows[strip + 1, g] = staged[:, :, STRIP:2 * STRIP]
+            nc.sync.dma_start(out=staged[:], in_=rows.rearrange("(p j) w -> p j w", j=PACK))
 
         def load_g_scales(h):
-            dst = g_plane[h][:].bitcast(I32).rearrange("p (g w) -> p g w", g=PASSES)
-            src = g_scales.rearrange("g (q r) n -> r q g n", r=4)
-            for r in range(4):
-                nc.sync.dma_start(out=dst[r:P:32], in_=src[r][:, :, h * NH:(h + 1) * NH].bitcast(I32))
+            dst = g_scale_tiles[h][:].bitcast(I32).rearrange("p (g w) -> p g w", g=PASSES)
+            src = g_scales.rearrange("g (q r) n -> r q g n", r=SCALE_ROWS)
+            for r in range(SCALE_ROWS):
+                nc.sync.dma_start(out=dst[r:P:32], in_=src[r][:, :, h * HALF:(h + 1) * HALF].bitcast(I32))
 
-        def interleave(on_vector, strip, g, c0, width):
-            first = (strip % 2) * STRIP + c0
-            src = raw[strip // 2, g][:, :, first:first + width].rearrange("p t (c i) -> p c t i", i=4)
-            dst = grouped[strip, g][:, c0:c0 + width, :].rearrange("p (c i) t -> p c t i", i=4)
-            if on_vector:
-                nc.vector.tensor_copy(out=dst, in_=src)
-            else:
-                nc.scalar.copy(out=dst, in_=src)
+        def lay_side_by_side(strip, g):
+            for u in range(2):
+                cols = slice(u * P, (u + 1) * P)
+                src = jac_rows[strip, g][:, :, cols].rearrange("p j (c i) -> p c j i", i=RUN)
+                dst = side_by_side[strip, g][:, cols, :].rearrange("p (c i) j -> p c j i", i=RUN)
+                if u == 0:
+                    nc.vector.tensor_copy(out=dst, in_=src)
+                else:
+                    nc.scalar.copy(out=dst, in_=src)
 
         def quantize(strip, g):
             nc.vector.quantize_mx(
-                out=j_codes[strip, g][:].bitcast(E4M3X4),
-                scales=j_scales[strip, g][:],
-                in_=grouped[strip, g][:].rearrange("p c t -> p (c t)"),
+                out=jac_codes[strip, g][:].bitcast(E4M3X4),
+                scales=jac_scales[strip, g][:],
+                in_=side_by_side[strip, g][:].rearrange("p c j -> p (c j)"),
             )
 
         def multiply(i, g):
@@ -103,120 +105,113 @@ def tile_committee_descriptor_forces_e1_kernel(tc, g_words, g_scales, jac, e_sca
             cols = slice((t % 2) * P, (t % 2 + 1) * P)
             nc.tensor.matmul_mx(
                 out=banks[i % BANKS][:],
-                lhsT=j_codes[t // 2, g][:, cols].bitcast(E4M3X4),
-                lhsT_scale=j_scales[t // 2, g][:, cols],
+                lhsT=jac_codes[t // 2, g][:, cols].bitcast(E4M3X4),
+                lhsT_scale=jac_scales[t // 2, g][:, cols],
                 rhs=g_codes[g, h].bitcast(E5M2X4),
-                rhs_scale=g_plane[h][:, g * NH:(g + 1) * NH],
+                rhs_scale=g_scale_tiles[h][:, g * HALF:(g + 1) * HALF],
                 start=(g == 0),
                 stop=(g == PASSES - 1),
             )
 
-        def scale_out(i):
-            nc.vector.tensor_tensor(out=res[i], in0=banks[i % BANKS][:], in1=neg_e[groups[i][1]][:], op=ALU.mult)
+        def multiply_group(i):
+            for g in range(PASSES):
+                multiply(i, g)
 
-        def finish(i):
+        def empty_bank(i, cols):
+            nc.vector.tensor_tensor(
+                out=results[i][:, cols], in0=banks[i % BANKS][:, cols], in1=neg_e[groups[i][1]][:, cols], op=ALU.mult
+            )
+
+        def add_base_and_store(i):
             t, h = groups[i]
-            if i in VECTOR_ADDS:
-                nc.vector.tensor_scalar_add(out=res[i], in0=res[i], scalar1=base_cols[:, t:t + 1])
-            else:
-                nc.scalar.activation(out=res[i], in_=res[i], func=ACT.Identity, bias=base_cols[:, t:t + 1])
-            if i >= len(groups) - SINGLE_STORES:
-                nc.sync.dma_start(out=out[t * P:(t + 1) * P, h * NH:(h + 1) * NH], in_=res[i])
+            nc.scalar.activation(out=results[i], in_=results[i], func=ACT.Identity, bias=base_cols[:, t:t + 1])
+            if i > last - SINGLE_STORES:
+                nc.sync.dma_start(out=out[t * P:(t + 1) * P, h * HALF:(h + 1) * HALF], in_=results[i])
             elif i % 2 == 1 and i < 2 * BANKS:
-                rows = out[(t - 1) * P:(t + 1) * P, h * NH:(h + 1) * NH]
+                rows = out[(t - 1) * P:(t + 1) * P, h * HALF:(h + 1) * HALF]
                 nc.sync.dma_start(out=rows.rearrange("(u p) n -> p u n", p=P), in_=pairs[i // 2][:])
             elif i % 2 == 1:
                 nc.sync.dma_start(out=out[t * P:(t + 1) * P, :], in_=pairs[i // 2][:].rearrange("p u n -> p (u n)"))
 
-        nc.scalar.dma_start(out=e_rows[:], in_=e_scale.rearrange("(h q m) -> q h m", h=2, m=PACK))
-        nc.vector.memset(one[:], 1.0)
+        nc.scalar.dma_start(out=e_parts[:], in_=e_scale.rearrange("(h q m) -> q h m", h=2, m=PACK))
         nc.vector.memset(base_rows[:], 0.0)
+        nc.vector.memset(one[:], 1.0)
+        nc.gpsimd.dma_start(out=base_rows[0:TILES, :], in_=base.rearrange("(t p) -> t p", p=P))
         nc.scalar.activation(out=minus_one[:], in_=one[:], func=ACT.Identity, scale=-1.0)
-        nc.gpsimd.dma_start(out=base_rows[0:C // P, :], in_=base.rearrange("(t p) -> t p", p=P))
         for h in range(2):
-            nc.vector.memset(g_plane[h][:].bitcast(I32), 0)
+            nc.vector.memset(g_scale_tiles[h][:].bitcast(I32), 0)
         make_identity(nc, ident[:])
 
         for g in range(PASSES):
-            load_jac(0, g)
-            load_jac(1, g)
+            load_strip_pair(0, g)
             if g == 0:
                 load_g_scales(0)
-            load_g(g)
+            load_strip_pair(2, g)
+            nc.sync.dma_start(out=g_codes[g, 0].bitcast(I32), in_=g_word_rows[:, g, 0:HALF])
         load_g_scales(1)
         for g in range(0, PASSES, 2):
-            nc.sync.dma_start(out=g_late[:, g:g + 2, :].bitcast(I32), in_=g_rows[:, g:g + 2, NH:N])
+            nc.sync.dma_start(out=g_second[:, g:g + 2, :].bitcast(I32), in_=g_word_rows[:, g:g + 2, HALF:N])
         for g in range(PASSES):
-            load_jac(2, g)
+            load_strip_pair(FIRST_STRIPS, g)
 
-        spread = [banks[BANKS - 2 + h][:].bitcast(BF16) for h in range(2)]
+        turned = [banks[BANKS - 2 + h][:].bitcast(BF16) for h in range(2)]
         for h in range(2):
             for m in range(PACK):
                 nc.tensor.transpose(
-                    spread[h][:, m * P:(m + 1) * P], e_rows[:, h, m:m + 1].to_broadcast([P, P]), ident[:]
+                    turned[h][:, m * P:(m + 1) * P], e_parts[:, h, m:m + 1].to_broadcast([P, P]), ident[:]
                 )
-        nc.tensor.transpose(spread[0][:, NH:NH + P], base_rows[:], ident[:])
+        nc.tensor.transpose(turned[0][:, HALF:HALF + P], base_rows[:], ident[:])
 
-        def fetch_constants():
-            e_src = [spread[h][:, 0:NH].rearrange("p (m q) -> p q m", m=PACK) for h in range(2)]
-            e_dst = [neg_e[h][:].rearrange("p (q m) -> p q m", m=PACK) for h in range(2)]
-            nc.vector.tensor_scalar_mul(out=e_dst[0], in0=e_src[0], scalar1=minus_one[:])
-            nc.scalar.activation(out=e_dst[1], in_=e_src[1], func=ACT.Identity, scale=minus_one[:])
-            nc.vector.tensor_copy(out=base_cols[:], in_=spread[0][:, NH:NH + C // P])
-
-        def multiply_strip(strip, g):
-            multiply(2 * strip, g)
-            multiply(2 * strip + 1, g)
+        def copy_out_constants():
+            src = [turned[h][:, 0:HALF].rearrange("p (m q) -> p q m", m=PACK) for h in range(2)]
+            dst = [neg_e[h][:].rearrange("p (q m) -> p q m", m=PACK) for h in range(2)]
+            nc.vector.tensor_scalar_mul(out=dst[0], in0=src[0], scalar1=minus_one[:])
+            nc.scalar.activation(out=dst[1], in_=src[1], func=ACT.Identity, scale=minus_one[:])
+            nc.vector.tensor_copy(out=base_cols[:], in_=turned[0][:, HALF:HALF + TILES])
 
         for g in range(PASSES):
-            interleave(True, 0, g, 0, STRIP)
-            interleave(False, 1, g, 0, STRIP)
-            quantize(0, g)
-            interleave(True, 2, g, 0, STRIP)
-            interleave(False, 3, g, 0, STRIP)
-            quantize(1, g)
-            quantize(2, g)
-            if g == 0:
-                fetch_constants()
-            quantize(3, g)
-            for strip in range(4):
-                multiply_strip(strip, g)
+            lay_side_by_side(0, g)
+            for strip in range(FIRST_STRIPS):
+                if strip + 1 < FIRST_STRIPS:
+                    lay_side_by_side(strip + 1, g)
+                elif g == 0:
+                    copy_out_constants()
+                quantize(strip, g)
+                multiply(2 * strip, g)
+                multiply(2 * strip + 1, g)
 
-        late = [(strip, g) for strip in (4, 5) for g in range(PASSES)]
-        last = len(groups) - 1
-        issued = BANKS
-        quantized = set((strip, PASSES - 1) for strip in range(4))
+        late = [(strip, g) for strip in range(FIRST_STRIPS, STRIPS) for g in range(PASSES)]
         for i in range(last + ADD_LAG):
-            prepare = i in PREP_STEPS
-            if prepare:
-                j = PREP_STEPS.index(i)
-                interleave(True, late[j][0], late[j][1], 0, LATE_SPLIT)
-                interleave(False, late[j][0], late[j][1], LATE_SPLIT, STRIP - LATE_SPLIT)
+            prepares = BANKS <= i < BANKS + len(late)
+            if prepares:
+                lay_side_by_side(*late[i - BANKS])
             if i < last:
-                scale_out(i)
-            if prepare:
-                quantize(*late[j])
-                quantized.add(late[j])
-            if i >= ADD_LAG and i - ADD_LAG not in VECTOR_ADDS:
-                finish(i - ADD_LAG)
-            if i - 1 in VECTOR_ADDS:
-                finish(i - 1)
-            while issued <= min(i + BANKS, last) and (groups[issued][0] // 2, PASSES - 1) in quantized:
+                empty_bank(i, slice(0, HALF))
+            if prepares:
+                quantize(*late[i - BANKS])
+            if i >= ADD_LAG:
+                add_base_and_store(i - ADD_LAG)
+            if i == OPENING_GROUPS - 1:
                 for g in range(PASSES):
-                    multiply(issued, g)
-                issued += 1
+                    for k in range(OPENING_GROUPS):
+                        multiply(BANKS + k, g)
+            elif OPENING_GROUPS <= i < BANKS:
+                multiply_group(BANKS + i)
+            elif prepares and late[i - BANKS][1] == PASSES - 1:
+                for k in range(len(groups)):
+                    if groups[k][0] // 2 == late[i - BANKS][0]:
+                        multiply_group(k)
 
         t, h = groups[last]
-        for u in range(2):
-            cols = slice(u * NH // 2, (u + 1) * NH // 2)
-            nc.vector.tensor_tensor(out=res[last][:, cols], in0=banks[last % BANKS][:, cols], in1=neg_e[h][:, cols], op=ALU.mult)
-        for u in range(2):
-            cols = slice(u * NH // 2, (u + 1) * NH // 2)
-            part = res[last][:, cols]
-            rows = out[t * P:(t + 1) * P, h * NH + cols.start:h * NH + cols.stop]
-            if u == 0:
-                nc.scalar.activation(out=part, in_=part, func=ACT.Identity, bias=base_cols[:, t:t + 1])
-                nc.scalar.dma_start(out=rows, in_=part)
-            else:
-                nc.vector.tensor_scalar_add(out=part, in0=part, scalar1=base_cols[:, t:t + 1])
-                nc.sync.dma_start(out=rows, in_=part)
+        left, right = slice(0, HALF // 2), slice(HALF // 2, HALF)
+        out_last = out[t * P:(t + 1) * P, h * HALF:(h + 1) * HALF]
+        empty_bank(last, left)
+        empty_bank(last, right)
+        nc.scalar.activation(
+            out=results[last][:, left], in_=results[last][:, left], func=ACT.Identity, bias=base_cols[:, t:t + 1]
+        )
+        nc.scalar.dma_start(out=out_last[:, left], in_=results[last][:, left])
+        nc.vector.tensor_scalar_add(
+            out=results[last][:, right], in0=results[last][:, right], scalar1=base_cols[:, t:t + 1]
+        )
+        nc.sync.dma_start(out=out_last[:, right], in_=results[last][:, right])

from contextlib import ExitStack

import concourse.mybir as mybir
from concourse.masks import make_identity

K, C, N = 2048, 1536, 1024
FLOPS = 2 * K * C * N

F32 = mybir.dt.float32
BF16 = mybir.dt.bfloat16
I32 = mybir.dt.int32
U32 = mybir.dt.uint32
U8 = mybir.dt.uint8
E4M3X4 = mybir.dt.float8_e4m3fn_x4
E5M2X4 = mybir.dt.float8_e5m2_x4
ACT = mybir.ActivationFunctionType
ALU = mybir.AluOpType

P = 128
PACK = 4
K_PASS = P * PACK
PASSES = K // K_PASS
TILES = C // P
STRIP = 2 * P
STRIPS = C // STRIP
HALF = N // 2
BANKS = 8
FIRST_STRIPS = BANKS // 2
RUN = 4
SCALE_ROWS = 4
ADD_LAG = 2
OPENING_GROUPS = 2
SINGLE_STORES = 4


def tile_committee_descriptor_forces_e1_kernel(tc, g_words, g_scales, jac, e_scale, base, out):
    nc = tc.nc
    with ExitStack() as ctx:
        sb = ctx.enter_context(tc.tile_pool(name="sb", bufs=1))
        ps = ctx.enter_context(tc.psum_pool(name="ps", bufs=1))
        ctx.enter_context(tc.manual_schedule())

        banks = [ps.tile([P, HALF], F32, name="bank%d" % b) for b in range(BANKS)]
        jac_rows, side_by_side, jac_codes, jac_scales = {}, {}, {}, {}
        for strip in range(STRIPS):
            for g in range(PASSES):
                key = (strip, g)
                side_by_side[key] = sb.tile([P, STRIP, PACK], BF16, name="side%d_%d" % key, align_bytes=64)
                jac_codes[key] = sb.tile([P, STRIP], U32, name="jcode%d_%d" % key, align_bytes=64)
                jac_scales[key] = sb.tile([P, STRIP], U8, name="jscale%d_%d" % key, align_bytes=64)
        g_second = sb.tile([P, PASSES, HALF], U32, align_bytes=64)
        g_codes = {}
        for g in range(PASSES):
            g_codes[g, 0] = sb.tile([P, HALF], U32, name="gfirst%d" % g, align_bytes=64)[:]
            g_codes[g, 1] = g_second[:, g, :]
        g_scale_tiles = [sb.tile([P, PASSES * HALF], U8, name="gscale%d" % h, align_bytes=64) for h in range(2)]
        neg_e = [sb.tile([P, HALF], F32, name="nege%d" % h) for h in range(2)]
        e_parts = sb.tile([P, 2, PACK], BF16)
        base_rows = sb.tile([P, P], BF16)
        base_cols = sb.tile([P, TILES], F32)
        one = sb.tile([P, 1], F32)
        minus_one = sb.tile([P, 1], F32)
        ident = sb.tile([P, P], BF16)

        groups = [(t, 0) for t in range(BANKS)] + [(t, 1) for t in range(BANKS)]
        groups += [(t, h) for t in range(BANKS, TILES) for h in range(2)]
        last = len(groups) - 1
        pairs = [sb.tile([P, 2, HALF], F32, name="result%d" % u) for u in range(len(groups) // 2)]
        results = [pairs[i // 2][:, i % 2, :] for i in range(len(groups))]

        g_word_rows = g_words.rearrange("g p n j -> p g (n j)").bitcast(I32)

        def load_strip_pair(strip, g):
            rows = jac[g * K_PASS:(g + 1) * K_PASS, strip * STRIP:(strip + 2) * STRIP]
            staged = sb.tile([P, PACK, 2 * STRIP], BF16, name="rows%d_%d" % (strip, g), align_bytes=64)
            jac_rows[strip, g] = staged[:, :, 0:STRIP]
            jac_rows[strip + 1, g] = staged[:, :, STRIP:2 * STRIP]
            nc.sync.dma_start(out=staged[:], in_=rows.rearrange("(p j) w -> p j w", j=PACK))

        def load_g_scales(h):
            dst = g_scale_tiles[h][:].bitcast(I32).rearrange("p (g w) -> p g w", g=PASSES)
            src = g_scales.rearrange("g (q r) n -> r q g n", r=SCALE_ROWS)
            for r in range(SCALE_ROWS):
                nc.sync.dma_start(out=dst[r:P:32], in_=src[r][:, :, h * HALF:(h + 1) * HALF].bitcast(I32))

        def lay_side_by_side(strip, g):
            for u in range(2):
                cols = slice(u * P, (u + 1) * P)
                src = jac_rows[strip, g][:, :, cols].rearrange("p j (c i) -> p c j i", i=RUN)
                dst = side_by_side[strip, g][:, cols, :].rearrange("p (c i) j -> p c j i", i=RUN)
                if u == 0:
                    nc.vector.tensor_copy(out=dst, in_=src)
                else:
                    nc.scalar.copy(out=dst, in_=src)

        def quantize(strip, g):
            nc.vector.quantize_mx(
                out=jac_codes[strip, g][:].bitcast(E4M3X4),
                scales=jac_scales[strip, g][:],
                in_=side_by_side[strip, g][:].rearrange("p c j -> p (c j)"),
            )

        def multiply(i, g):
            t, h = groups[i]
            cols = slice((t % 2) * P, (t % 2 + 1) * P)
            nc.tensor.matmul_mx(
                out=banks[i % BANKS][:],
                lhsT=jac_codes[t // 2, g][:, cols].bitcast(E4M3X4),
                lhsT_scale=jac_scales[t // 2, g][:, cols],
                rhs=g_codes[g, h].bitcast(E5M2X4),
                rhs_scale=g_scale_tiles[h][:, g * HALF:(g + 1) * HALF],
                start=(g == 0),
                stop=(g == PASSES - 1),
            )

        def multiply_group(i):
            for g in range(PASSES):
                multiply(i, g)

        def empty_bank(i, cols):
            nc.vector.tensor_tensor(
                out=results[i][:, cols], in0=banks[i % BANKS][:, cols], in1=neg_e[groups[i][1]][:, cols], op=ALU.mult
            )

        def add_base_and_store(i):
            t, h = groups[i]
            nc.scalar.activation(out=results[i], in_=results[i], func=ACT.Identity, bias=base_cols[:, t:t + 1])
            if i > last - SINGLE_STORES:
                nc.sync.dma_start(out=out[t * P:(t + 1) * P, h * HALF:(h + 1) * HALF], in_=results[i])
            elif i % 2 == 1 and i < 2 * BANKS:
                rows = out[(t - 1) * P:(t + 1) * P, h * HALF:(h + 1) * HALF]
                nc.sync.dma_start(out=rows.rearrange("(u p) n -> p u n", p=P), in_=pairs[i // 2][:])
            elif i % 2 == 1:
                nc.sync.dma_start(out=out[t * P:(t + 1) * P, :], in_=pairs[i // 2][:].rearrange("p u n -> p (u n)"))

        nc.scalar.dma_start(out=e_parts[:], in_=e_scale.rearrange("(h q m) -> q h m", h=2, m=PACK))
        nc.vector.memset(base_rows[:], 0.0)
        nc.vector.memset(one[:], 1.0)
        nc.gpsimd.dma_start(out=base_rows[0:TILES, :], in_=base.rearrange("(t p) -> t p", p=P))
        nc.scalar.activation(out=minus_one[:], in_=one[:], func=ACT.Identity, scale=-1.0)
        for h in range(2):
            nc.vector.memset(g_scale_tiles[h][:].bitcast(I32), 0)
        make_identity(nc, ident[:])

        for g in range(PASSES):
            load_strip_pair(0, g)
            if g == 0:
                load_g_scales(0)
            load_strip_pair(2, g)
            nc.sync.dma_start(out=g_codes[g, 0].bitcast(I32), in_=g_word_rows[:, g, 0:HALF])
        load_g_scales(1)
        for g in range(0, PASSES, 2):
            nc.sync.dma_start(out=g_second[:, g:g + 2, :].bitcast(I32), in_=g_word_rows[:, g:g + 2, HALF:N])
        for g in range(PASSES):
            load_strip_pair(FIRST_STRIPS, g)

        turned = [banks[BANKS - 2 + h][:].bitcast(BF16) for h in range(2)]
        for h in range(2):
            for m in range(PACK):
                nc.tensor.transpose(
                    turned[h][:, m * P:(m + 1) * P], e_parts[:, h, m:m + 1].to_broadcast([P, P]), ident[:]
                )
        nc.tensor.transpose(turned[0][:, HALF:HALF + P], base_rows[:], ident[:])

        def copy_out_constants():
            src = [turned[h][:, 0:HALF].rearrange("p (m q) -> p q m", m=PACK) for h in range(2)]
            dst = [neg_e[h][:].rearrange("p (q m) -> p q m", m=PACK) for h in range(2)]
            nc.vector.tensor_scalar_mul(out=dst[0], in0=src[0], scalar1=minus_one[:])
            nc.scalar.activation(out=dst[1], in_=src[1], func=ACT.Identity, scale=minus_one[:])
            nc.vector.tensor_copy(out=base_cols[:], in_=turned[0][:, HALF:HALF + TILES])

        for g in range(PASSES):
            lay_side_by_side(0, g)
            for strip in range(FIRST_STRIPS):
                if strip + 1 < FIRST_STRIPS:
                    lay_side_by_side(strip + 1, g)
                elif g == 0:
                    copy_out_constants()
                quantize(strip, g)
                multiply(2 * strip, g)
                multiply(2 * strip + 1, g)

        late = [(strip, g) for strip in range(FIRST_STRIPS, STRIPS) for g in range(PASSES)]
        for i in range(last + ADD_LAG):
            prepares = BANKS <= i < BANKS + len(late)
            if prepares:
                lay_side_by_side(*late[i - BANKS])
            if i < last:
                empty_bank(i, slice(0, HALF))
            if prepares:
                quantize(*late[i - BANKS])
            if i >= ADD_LAG:
                add_base_and_store(i - ADD_LAG)
            if i == OPENING_GROUPS - 1:
                for g in range(PASSES):
                    for k in range(OPENING_GROUPS):
                        multiply(BANKS + k, g)
            elif OPENING_GROUPS <= i < BANKS:
                multiply_group(BANKS + i)
            elif prepares and late[i - BANKS][1] == PASSES - 1:
                for k in range(len(groups)):
                    if groups[k][0] // 2 == late[i - BANKS][0]:
                        multiply_group(k)

        t, h = groups[last]
        left, right = slice(0, HALF // 2), slice(HALF // 2, HALF)
        out_last = out[t * P:(t + 1) * P, h * HALF:(h + 1) * HALF]
        empty_bank(last, left)
        empty_bank(last, right)
        nc.scalar.activation(
            out=results[last][:, left], in_=results[last][:, left], func=ACT.Identity, bias=base_cols[:, t:t + 1]
        )
        nc.scalar.dma_start(out=out_last[:, left], in_=results[last][:, left])
        nc.vector.tensor_scalar_add(
            out=results[last][:, right], in0=results[last][:, right], scalar1=base_cols[:, t:t + 1]
        )
        nc.sync.dma_start(out=out_last[:, right], in_=results[last][:, right])
